import numpy as np
import ml_dtypes


def mxq(x, axis, fmt="e4m3"):
    dtype, down = {"e4m3": (ml_dtypes.float8_e4m3fn, 7), "e5m2": (ml_dtypes.float8_e5m2, 14)}[fmt]
    v = np.moveaxis(np.asarray(x, np.float32).astype(ml_dtypes.bfloat16).astype(np.float64), axis, -1)
    blocks = v.reshape(v.shape[:-1] + (-1, 32))
    amax = np.abs(blocks).max(-1, keepdims=True)
    byte = np.maximum(np.where(amax > 0, np.frexp(amax)[1] - 1 + 127, 0) - down, 1)
    scale = np.exp2(byte - 127.0)
    codes = (blocks / scale).astype(np.float32).astype(dtype).astype(np.float64)
    return np.moveaxis((codes * scale).reshape(v.shape), -1, axis)


WIDE = False


def mx_kscale(k):
    if not WIDE:
        return np.ones(k)
    levels = np.array([24, -24, 12, -12, 0])
    if k % 512:
        return np.exp2(np.random.permutation(np.resize(levels, k // 32))).repeat(32)
    a = np.empty((k // 512, 16))
    for p in range(k // 512):
        a[p, :8] = np.random.permutation(np.resize(levels, 8))
        for g in range(8):
            far = levels[np.abs(levels - a[p, g]) >= 10]
            a[p, g + 8] = far[np.random.randint(len(far))]
    return np.exp2(a.ravel()).repeat(32)


def f64(x):
    return np.asarray(x).astype(np.float64)


def striped(idx):
    return np.tile(idx.reshape(-1, 16).T, (8, 1)).astype(np.uint16)


def unstriped(offs):
    return offs[:16].T.reshape(-1).astype(np.int64)


E2M1 = np.array([0.0, 0.5, 1.0, 1.5, 2.0, 3.0, 4.0, 6.0, -0.0, -0.5, -1.0, -1.5, -2.0, -3.0, -4.0, -6.0])


def pack_weight(w, fmt):
    k, n = w.shape
    w = f64(np.asarray(w, np.float32).astype(ml_dtypes.bfloat16)).reshape(k // 32, 32, n)
    amax = np.abs(w).max(1)
    if fmt == "e4m3":
        byte = np.frexp(amax)[1] - 1 + 127 - 7
    else:
        mant, ex = np.frexp(amax / 6.0)
        byte = np.where(mant > 0.5, ex, ex - 1) + 127
    byte = np.clip(np.where(amax > 0, byte, 1), 1, 254)
    scaled = (w * np.exp2(127.0 - byte)[:, None, :]).reshape(k, n).astype(np.float32)
    by_word = np.ascontiguousarray(scaled.reshape(k // 512, 128, 4, n).transpose(0, 1, 3, 2))
    if fmt == "e4m3":
        words = by_word.astype(ml_dtypes.float8_e4m3fn).view(np.uint8)
    else:
        c = by_word.astype(ml_dtypes.float4_e2m1fn).view(np.uint8) & 0xF
        words = (c[..., 0::2] | (c[..., 1::2] << 4)).reshape(k // 512, 128, 2 * n)
    return np.ascontiguousarray(words), np.ascontiguousarray(byte.astype(np.uint8).reshape(k // 512, 16, n))


def unpack_weight(words, scales, fmt):
    g, _, n = scales.shape
    words = np.ascontiguousarray(words).reshape(g, 128, n, -1)
    if fmt == "e4m3":
        vals = words.view(ml_dtypes.float8_e4m3fn).astype(np.float64)
    else:
        nib = np.empty((g, 128, n, 4), np.uint8)
        nib[..., 0::2] = words & 0xF
        nib[..., 1::2] = words >> 4
        vals = E2M1[nib]
    vals = vals * np.repeat(np.exp2(scales.astype(np.float64) - 127.0), 8, axis=1)[..., None]
    return vals.transpose(0, 1, 3, 2).reshape(g * 512, n)


def sigm(f):
    return 1.0 / (1.0 + np.exp(-np.maximum(f, -700.0)))


K, N, T, J = 1024, 512, 2048, 1024


def setup_inputs():
    n = np.random.standard_normal
    s = mx_kscale(K)[:, None]
    p_tab = pack_weight(n((K, T)) * s, "e4m3")
    p_wb = pack_weight(n((K, N)) / np.sqrt(2 * K) / s, "e4m3")
    p_wc = pack_weight(n((K, N)) / np.sqrt(K) / s, "e4m3")
    return {
        "tab_words": p_tab[0],
        "tab_scales": p_tab[1],
        "wa": (n((K, N)) / np.sqrt(2 * K) / s).astype(np.float32),
        "wb_words": p_wb[0],
        "wb_scales": p_wb[1],
        "wc_words": p_wc[0],
        "wc_scales": p_wc[1],
        "wo": (n((K, N)) / np.sqrt(K) / s).astype(np.float32),
        "wgo": np.tile(np.random.uniform(0.5, 2.0, J), (128, 1)).astype(np.float32),
        "offs": striped(np.random.permutation(T)[:J]),
        "offs2": striped(np.random.permutation(T)[:J]),
    }


def reference(tab_words, tab_scales, wa, wb_words, wb_scales, wc_words, wc_scales, wo, wgo, offs, offs2):
    idx = unstriped(offs)
    idx2 = unstriped(offs2)
    tab_ = unpack_weight(tab_words, tab_scales, "e4m3")[:, idx]
    tabb_ = unpack_weight(tab_words, tab_scales, "e4m3")[:, idx2]
    wa_ = mxq(f64(wa), 0, "e4m3")
    wb_ = unpack_weight(wb_words, wb_scales, "e4m3")
    za = wa_.T @ tabb_ + wb_.T @ tab_
    eta = sigm(za)
    wc_ = unpack_weight(wc_words, wc_scales, "e4m3")
    ms = wc_.T @ tab_
    wo_ = mxq(f64(wo), 0, "e4m3")
    ow = wo_.T @ tabb_
    out = np.zeros((N, T))
    out[:, idx2] = f64(wgo)[0] * (np.maximum(ow + eta * ms, 0.0))
    return out

@@ -1,0 +1,208 @@
+from contextlib import ExitStack
+
+import concourse.mybir as mybir
+
+K, N, T, J = 1024, 512, 2048, 1024
+FLOPS = 4 * 2 * K * N * J
+
+F32 = mybir.dt.float32
+BF16 = mybir.dt.bfloat16
+I32 = mybir.dt.int32
+U32 = mybir.dt.uint32
+U16 = mybir.dt.uint16
+U8 = mybir.dt.uint8
+FP8X4 = mybir.dt.float8_e4m3fn_x4
+ACT = mybir.ActivationFunctionType
+ALU = mybir.AluOpType
+
+P = 128
+PASSES = 2
+JH = 512
+NH = 256
+
+
+def tile_list_rgg_ownrelu_kernel(
+    tc, tab_words, tab_scales, wa, wb_words, wb_scales, wc_words, wc_scales, wo, wgo, offs, offs2, out
+):
+    nc = tc.nc
+    with ExitStack() as ctx:
+        keep = ctx.enter_context(tc.tile_pool(name="keep", bufs=1))
+        work = ctx.enter_context(tc.tile_pool(name="work", bufs=3))
+        psum = ctx.enter_context(tc.psum_pool(name="psum", bufs=1))
+
+        lists = {"src": keep.tile([P, J // 16], U16, name="list_src"), "dst": keep.tile([P, J // 16], U16, name="list_dst")}
+        tab_s = keep.tile([P, T // 4], I32, name="tab_s", align_bytes=64)
+        wbc_s = keep.tile([P, 2, N // 4], I32, name="wbc_s", align_bytes=64)
+        tab_w = [keep.tile([P, T], I32, name="tab_w%d" % a, align_bytes=64) for a in range(PASSES)]
+        windows = [keep.tile([P, T], F32, name="window%d" % i, align_bytes=64) for i in range(3)]
+        wgo_sb = keep.tile([P, J], F32, name="wgo_sb", align_bytes=64)
+        warm = keep.tile([P, 8], F32, name="warm")
+
+        nc.vector.memset(tab_s[:], 0)
+        nc.sync.dma_start(lists["dst"][:], offs2)
+        nc.sync.dma_start(lists["src"][:], offs)
+        for q in range(4):
+            nc.sync.dma_start(tab_s[32 * q : 32 * q + 8, :], tab_scales[:, 4 * q : 4 * q + 4, :].bitcast(I32))
+        nc.vector.memset(wbc_s[:], 0)
+        nc.vector.memset(windows[0][:], 0.0)
+        nc.scalar.activation(warm[:], windows[0][:, 0:8], ACT.Sigmoid)
+        for i in range(1, 3):
+            nc.vector.memset(windows[i][:], 0.0)
+
+        def load_table(a):
+            nc.sync.dma_start(tab_w[a][:], tab_words[a].rearrange("p t i -> p (t i)").bitcast(I32))
+
+        raw, grouped, codes, planes = {}, {}, {}, {}
+
+        def load_float(name, w, g):
+            for a in range(PASSES):
+                t = keep.tile([P, 4, NH], F32, name="raw_%s%d%d" % (name, g, a), align_bytes=64)
+                raw[name, g, a] = t
+                nc.sync.dma_start(t[:], w[512 * a : 512 * (a + 1), NH * g : NH * (g + 1)].rearrange("(p i) n -> p i n", i=4))
+
+        def cast(name, g):
+            for a in range(PASSES):
+                t = keep.tile([P, NH, 4], BF16, name="grp_%s%d%d" % (name, g, a), align_bytes=64)
+                grouped[name, g, a] = t
+                nc.scalar.copy(
+                    t[:].rearrange("p (c e) i -> p c i e", e=4),
+                    raw[name, g, a][:].rearrange("p i (c e) -> p c i e", e=4),
+                )
+
+        def quantise(name, g):
+            for a in range(PASSES):
+                c = keep.tile([P, NH], U32, name="code_%s%d%d" % (name, g, a), align_bytes=64)
+                s = keep.tile([P, NH], U8, name="plane_%s%d%d" % (name, g, a), align_bytes=64)
+                nc.vector.quantize_mx(c[:].bitcast(FP8X4), s[:], grouped[name, g, a][:].rearrange("p n i -> p (n i)"))
+                codes[name, g, a] = c[:]
+                planes[name, g, a] = s[:]
+
+        def load_packed(name, words, g):
+            t = keep.tile([P, PASSES, NH], I32, name="code_%s%d" % (name, g), align_bytes=64)
+            nc.sync.dma_start(t[:], words.rearrange("a p n i -> p a (n i)")[:, :, 4 * NH * g : 4 * NH * (g + 1)].bitcast(I32))
+            for a in range(PASSES):
+                codes[name, g, a] = t[:, a, :]
+
+        def load_packed_scales():
+            for w, (name, scales) in enumerate((("wb", wb_scales), ("wc", wc_scales))):
+                for q in range(4):
+                    nc.sync.dma_start(wbc_s[32 * q : 32 * q + 8, w, :], scales[:, 4 * q : 4 * q + 4, :].bitcast(I32))
+                for g in range(2):
+                    for a in range(PASSES):
+                        planes[name, g, a] = wbc_s[:, w, :].bitcast(U8)[4 * a : P, NH * g : NH * (g + 1)]
+
+        load_table(0)
+        load_float("wa", wa, 0)
+        load_table(1)
+        load_float("wo", wo, 0)
+        load_packed_scales()
+        load_packed("wb", wb_words, 0)
+        load_packed("wc", wc_words, 0)
+        nc.sync.dma_start(wgo_sb[:], wgo)
+        load_float("wa", wa, 1)
+        load_packed("wb", wb_words, 1)
+        load_packed("wc", wc_words, 1)
+        load_float("wo", wo, 1)
+
+        picked_w, picked_s = {}, {}
+
+        def offsets(which, h):
+            return lists[which][:, (JH // 16) * h : (JH // 16) * (h + 1)]
+
+        def gather_scales(which, h):
+            t = keep.tile([P, JH], U8, name="ps_%s%d" % (which, h), align_bytes=64)
+            picked_s[which, h] = t
+            nc.vector.tensor_copy(t[:], tab_s[:].bitcast(U8).indirect(offsets(which, h)))
+
+        def gather_words(which, a, h):
+            t = keep.tile([P, JH], U32, name="pw_%s%d%d" % (which, a, h), align_bytes=64)
+            picked_w[which, a, h] = t
+            nc.vector.tensor_copy(t[:], tab_w[a][:].bitcast(U32).indirect(offsets(which, h)))
+
+        for h in range(2):
+            for which in ("dst", "src"):
+                gather_scales(which, h)
+        cast("wa", 0)
+        cast("wo", 0)
+        for h in range(2):
+            for which in ("dst", "src"):
+                gather_words(which, 0, h)
+        quantise("wa", 0)
+        for which in ("dst", "src"):
+            gather_words(which, 1, 0)
+        quantise("wo", 0)
+        for which in ("dst", "src"):
+            gather_words(which, 1, 1)
+        cast("wa", 1)
+        cast("wo", 1)
+
+        def product(bank, terms, nt, h):
+            steps = [(name, which, a) for a in range(PASSES) for name, which in terms]
+            g, cols = nt // 2, slice(P * (nt % 2), P * (nt % 2 + 1))
+            for i, (name, which, a) in enumerate(steps):
+                nc.tensor.matmul_mx(
+                    bank[:],
+                    lhsT=codes[name, g, a][:, cols].bitcast(FP8X4),
+                    lhsT_scale=planes[name, g, a][:, cols],
+                    rhs=picked_w[which, a, h][:].bitcast(FP8X4),
+                    rhs_scale=picked_s[which, h][4 * a : P, :],
+                    start=(i == 0),
+                    stop=(i == len(steps) - 1),
+                )
+
+        units = [(0, 0), (1, 0), (0, 1), (1, 1), (2, 0), (2, 1), (3, 0), (3, 1)]
+        state = {}
+
+        def multiply(u):
+            nt, h = units[u]
+            za = psum.tile([P, JH], F32, name="za", tag="za", bufs=2)
+            ms = psum.tile([P, JH], F32, name="ms", tag="ms", bufs=3)
+            ow = psum.tile([P, JH], F32, name="ow", tag="ow", bufs=3)
+            product(za, (("wa", "dst"), ("wb", "src")), nt, h)
+            product(ms, (("wc", "src"),), nt, h)
+            product(ow, (("wo", "dst"),), nt, h)
+            eta = work.tile([P, JH], F32, name="eta")
+            nc.scalar.activation(eta[:], za[:], ACT.Sigmoid)
+            state[u] = (eta, ms, ow)
+
+        def gate(u):
+            eta, ms, ow = state[u]
+            msg = work.tile([P, JH], F32, name="msg")
+            nc.vector.tensor_tensor(msg[:], ms[:], eta[:], ALU.mult)
+            state[u] = (msg, ow)
+
+        def add(u):
+            msg, ow = state[u]
+            y = work.tile([P, JH], F32, name="y")
+            nc.vector.tensor_tensor(y[:], ow[:], msg[:], ALU.add)
+            state[u] = y
+
+        def weigh(u):
+            h = units[u][1]
+            r = work.tile([P, JH], F32, name="r")
+            nc.vector.scalar_tensor_tensor(r[:], state[u][:], 0.0, wgo_sb[:, JH * h : JH * (h + 1)], ALU.max, ALU.mult)
+            state[u] = r
+
+        def scatter(u):
+            nt, h = units[u]
+            win = windows[nt % 3]
+            nc.vector.tensor_copy(win[:].indirect(offsets("dst", h)), state[u][:])
+            if h == 1:
+                nc.sync.dma_start(out[P * nt : P * (nt + 1), :], win[:])
+
+        multiply(0)
+        multiply(1)
+        gate(0)
+        for u in range(len(units)):
+            if u + 2 < len(units):
+                if u == 2:
+                    quantise("wa", 1)
+                    quantise("wo", 1)
+                multiply(u + 2)
+            add(u)
+            if u + 1 < len(units):
+                gate(u + 1)
+            weigh(u)
+            if u > 0:
+                scatter(u - 1)
+        scatter(len(units) - 1)

@@ -1,6 +1,7 @@
 from contextlib import ExitStack
 
 import concourse.mybir as mybir
+from concourse.masks import make_identity
 
 K, N, T, J = 1024, 512, 2048, 1024
 FLOPS = 4 * 2 * K * N * J
@@ -18,191 +19,285 @@ ALU = mybir.AluOpType
 P = 128
 PASSES = 2
 JH = 512
-NH = 256
+UNITS = ((0, 0), (1, 0), (0, 1), (1, 1), (2, 0), (2, 1), (3, 0), (3, 1))
+
+STEPS = (('load_float', 'wa', 0, 2, 0), ('zero', 's_tab'), ('zero', 's_wb'), ('load_list', 'dst'), ('zero', 's_wc'), ('load_scales', 'tab', 0),
+ ('load_scales', 'tab', 3), ('load_scales', 'wb', 2), ('load_scales', 'tab', 2), ('load_scales', 'tab', 1), ('load_table', 0), ('cast', 'wa', 1, 0),
+ ('load_list', 'src'), ('load_scales', 'wc', 3), ('load_scales', 'wc', 2), ('load_float', 'wa', 0, 2, 1), ('cast', 'wa', 1, 1),
+ ('load_scales', 'wb', 0), ('gather_words', 'dst', 0, 0), ('load_scales', 'wc', 1), ('load_float', 'wo', 0, 2, 0), ('load_table', 1),
+ ('gather_words', 'src', 1, 0), ('cast', 'wa', 0, 1), ('gather_words', 'dst', 1, 0), ('gather_scales', 'src', 1), ('zero', 'window3'),
+ ('load_float', 'wa', 2, 2, 0), ('warm',), ('identity',), ('gather_scales', 'src', 0), ('gather_words', 'src', 0, 0), ('load_scales', 'wb', 1),
+ ('load_scales', 'wb', 3), ('load_weight_column',), ('load_packed', 'wb', 0, 2), ('cast', 'wa', 0, 0), ('quantise', 'wa', 0),
+ ('gather_scales', 'dst', 1), ('gather_words', 'src', 0, 1), ('cast', 'wa', 2, 0), ('load_float', 'wo', 0, 2, 1), ('load_packed', 'wc', 0, 2),
+ ('load_scales', 'wc', 0), ('gather_words', 'src', 1, 1), ('gather_scales', 'dst', 0), ('load_float', 'wa', 2, 2, 1), ('load_float', 'wo', 2, 2, 0),
+ ('cast', 'wo', 1, 0), ('cast', 'wo', 0, 0), ('cast', 'wo', 0, 1), ('cast', 'wo', 1, 1), ('quantise', 'wa', 1), ('gather_words', 'dst', 0, 1),
+ ('quantise', 'wo', 0), ('load_packed', 'wc', 2, 2), ('product', 'za', 0), ('evacuate', 'za', 0), ('product', 'ms', 2), ('cast', 'wa', 2, 1),
+ ('product', 'ms', 0), ('evacuate', 'ms', 0), ('quantise', 'wo', 1), ('gate', 0), ('product', 'za', 1), ('product', 'ms', 1), ('product', 'ow', 0),
+ ('evacuate', 'ms', 1), ('zero', 'window0'), ('evacuate', 'ms', 2), ('load_weight_rows',), ('evacuate', 'ow', 0), ('gather_words', 'dst', 1, 1),
+ ('add', 0), ('product', 'ow', 2), ('evacuate', 'za', 1), ('cast', 'wa', 3, 1), ('product', 'ow', 1), ('gate', 1), ('load_float', 'wo', 2, 2, 1),
+ ('evacuate', 'ow', 1), ('add', 1), ('load_packed', 'wb', 2, 2), ('spread_weights',), ('product', 'za', 2), ('evacuate', 'za', 2),
+ ('zero', 'window2'), ('zero', 'window1'), ('evacuate', 'ow', 2), ('gate', 2), ('rectify', 1), ('cast', 'wa', 3, 0), ('product', 'ms', 3),
+ ('cast', 'wo', 2, 0), ('quantise', 'wa', 2), ('cast', 'wo', 3, 1), ('quantise', 'wa', 3), ('rectify', 0), ('product', 'ms', 6), ('product', 'za', 3),
+ ('weigh', 0), ('scatter', 0), ('evacuate', 'ms', 3), ('weigh', 1), ('product', 'ms', 4), ('evacuate', 'za', 3), ('evacuate', 'ms', 4),
+ ('cast', 'wo', 3, 0), ('product', 'za', 4), ('evacuate', 'za', 4), ('product', 'ow', 3), ('cast', 'wo', 2, 1), ('add', 2), ('rectify', 2),
+ ('product', 'za', 6), ('scatter', 1), ('gate', 3), ('gate', 4), ('weigh', 2), ('evacuate', 'ow', 3), ('quantise', 'wo', 2), ('product', 'za', 5),
+ ('quantise', 'wo', 3), ('scatter', 2), ('product', 'ow', 6), ('evacuate', 'za', 6), ('evacuate', 'ms', 6), ('product', 'ow', 4), ('gate', 6),
+ ('evacuate', 'ow', 4), ('product', 'ms', 7), ('evacuate', 'ow', 6), ('evacuate', 'ms', 7), ('product', 'ms', 5), ('add', 4), ('product', 'ow', 5),
+ ('evacuate', 'za', 5), ('add', 6), ('product', 'ow', 7), ('product', 'za', 7), ('rectify', 4), ('evacuate', 'ow', 5), ('add', 3), ('rectify', 6),
+ ('evacuate', 'ms', 5), ('gate', 5), ('add', 5), ('weigh', 4), ('rectify', 5), ('rectify', 3), ('evacuate', 'za', 7), ('evacuate', 'ow', 7),
+ ('scatter', 4), ('gate', 7), ('weigh', 3), ('weigh', 5), ('add', 7), ('scatter', 3), ('rectify', 7), ('scatter', 5), ('weigh', 7), ('weigh', 6),
+ ('scatter', 6), ('scatter', 7))
+CHAINS = (('eta1', 'plane_wa2'), ('code_wa3', 'ow_sb5'), ('eta6', 'ms_sb7'), ('grp_wa1', 'raw_wo21'), ('grp_wa3', 'y2'), ('raw_wa01', 'grp_wo1'),
+ ('raw_wa21', 'r0'), ('eta3', 'ow_sb3'), ('ms_sb2', 'msg3'), ('grp_wa0', 'pw_src11'))
+BANKS = {'ms0': 0,
+ 'ms1': 5,
+ 'ms2': 4,
+ 'ms3': 6,
+ 'ms4': 4,
+ 'ms5': 5,
+ 'ms6': 1,
+ 'ms7': 2,
+ 'ow0': 2,
+ 'ow1': 4,
+ 'ow2': 1,
+ 'ow3': 4,
+ 'ow4': 0,
+ 'ow5': 0,
+ 'ow6': 5,
+ 'ow7': 4,
+ 'w_rows': 7,
+ 'za0': 1,
+ 'za1': 6,
+ 'za2': 0,
+ 'za3': 0,
+ 'za4': 2,
+ 'za5': 3,
+ 'za6': 0,
+ 'za7': 6}
+OPT = {'add0': 'V',
+ 'add1': 'V',
+ 'add2': 'G',
+ 'add3': 'G',
+ 'add4': 'V',
+ 'add5': 'G',
+ 'add6': 'G',
+ 'add7': 'G',
+ 'cast_wa00': 'S',
+ 'cast_wa01': 'S',
+ 'cast_wa10': 'S',
+ 'cast_wa11': 'S',
+ 'cast_wa20': 'S',
+ 'cast_wa21': 'S',
+ 'cast_wa30': 'S',
+ 'cast_wa31': 'G',
+ 'cast_wo00': 'G',
+ 'cast_wo01': 'G',
+ 'cast_wo10': 'S',
+ 'cast_wo11': 'S',
+ 'cast_wo20': 'S',
+ 'cast_wo21': 'S',
+ 'cast_wo30': 'S',
+ 'cast_wo31': 'S',
+ 'gate0': 'V',
+ 'gate1': 'V',
+ 'gate2': 'G',
+ 'gate3': 'G',
+ 'gate4': 'G',
+ 'gate5': 'G',
+ 'gate6': 'G',
+ 'gate7': 'G',
+ 'q_tab': 'SP',
+ 'q_wb': 'SP',
+ 'q_wc': 'SP',
+ 'q_wcol': 'SP',
+ 'q_wgo': 'SP',
+ 'weigh0': 'V',
+ 'weigh1': 'V',
+ 'weigh2': 'G',
+ 'weigh3': 'G',
+ 'weigh4': 'V',
+ 'weigh5': 'G',
+ 'weigh6': 'V',
+ 'weigh7': 'F',
+ 'zero_s_tab': 'V',
+ 'zero_s_wb': 'G',
+ 'zero_s_wc': 'V',
+ 'zero_window0': 'V',
+ 'zero_window1': 'G',
+ 'zero_window2': 'G',
+ 'zero_window3': 'V'}
 
 
 def tile_list_rgg_ownrelu_kernel(
     tc, tab_words, tab_scales, wa, wb_words, wb_scales, wc_words, wc_scales, wo, wgo, offs, offs2, out
 ):
     nc = tc.nc
+    engines = {"V": nc.vector, "G": nc.gpsimd, "S": nc.scalar, "SP": nc.sync}
     with ExitStack() as ctx:
         keep = ctx.enter_context(tc.tile_pool(name="keep", bufs=1))
-        work = ctx.enter_context(tc.tile_pool(name="work", bufs=3))
         psum = ctx.enter_context(tc.psum_pool(name="psum", bufs=1))
+        slot_of = {name: chain[0] for chain in CHAINS for name in chain}
+        tiles = {}
+
+        def sb(name, shape, dtype):
+            if name not in tiles:
+                tiles[name] = keep.tile(shape, dtype, name=name, tag=slot_of.get(name, name), align_bytes=64)
+            return tiles[name]
+
+        def bank(name):
+            tiles[name] = psum.tile([P, JH], F32, name=name, tag="bank%d" % BANKS[name])
+            return tiles[name]
 
         lists = {"src": keep.tile([P, J // 16], U16, name="list_src"), "dst": keep.tile([P, J // 16], U16, name="list_dst")}
-        tab_s = keep.tile([P, T // 4], I32, name="tab_s", align_bytes=64)
-        wbc_s = keep.tile([P, 2, N // 4], I32, name="wbc_s", align_bytes=64)
-        tab_w = [keep.tile([P, T], I32, name="tab_w%d" % a, align_bytes=64) for a in range(PASSES)]
-        windows = [keep.tile([P, T], F32, name="window%d" % i, align_bytes=64) for i in range(3)]
-        wgo_sb = keep.tile([P, J], F32, name="wgo_sb", align_bytes=64)
-        warm = keep.tile([P, 8], F32, name="warm")
-
-        nc.vector.memset(tab_s[:], 0)
-        nc.sync.dma_start(lists["dst"][:], offs2)
-        nc.sync.dma_start(lists["src"][:], offs)
-        for q in range(4):
-            nc.sync.dma_start(tab_s[32 * q : 32 * q + 8, :], tab_scales[:, 4 * q : 4 * q + 4, :].bitcast(I32))
-        nc.vector.memset(wbc_s[:], 0)
-        nc.vector.memset(windows[0][:], 0.0)
-        nc.scalar.activation(warm[:], windows[0][:, 0:8], ACT.Sigmoid)
-        for i in range(1, 3):
-            nc.vector.memset(windows[i][:], 0.0)
-
-        def load_table(a):
-            nc.sync.dma_start(tab_w[a][:], tab_words[a].rearrange("p t i -> p (t i)").bitcast(I32))
-
-        raw, grouped, codes, planes = {}, {}, {}, {}
-
-        def load_float(name, w, g):
-            for a in range(PASSES):
-                t = keep.tile([P, 4, NH], F32, name="raw_%s%d%d" % (name, g, a), align_bytes=64)
-                raw[name, g, a] = t
-                nc.sync.dma_start(t[:], w[512 * a : 512 * (a + 1), NH * g : NH * (g + 1)].rearrange("(p i) n -> p i n", i=4))
-
-        def cast(name, g):
-            for a in range(PASSES):
-                t = keep.tile([P, NH, 4], BF16, name="grp_%s%d%d" % (name, g, a), align_bytes=64)
-                grouped[name, g, a] = t
-                nc.scalar.copy(
-                    t[:].rearrange("p (c e) i -> p c i e", e=4),
-                    raw[name, g, a][:].rearrange("p i (c e) -> p c i e", e=4),
-                )
-
-        def quantise(name, g):
-            for a in range(PASSES):
-                c = keep.tile([P, NH], U32, name="code_%s%d%d" % (name, g, a), align_bytes=64)
-                s = keep.tile([P, NH], U8, name="plane_%s%d%d" % (name, g, a), align_bytes=64)
-                nc.vector.quantize_mx(c[:].bitcast(FP8X4), s[:], grouped[name, g, a][:].rearrange("p n i -> p (n i)"))
-                codes[name, g, a] = c[:]
-                planes[name, g, a] = s[:]
-
-        def load_packed(name, words, g):
-            t = keep.tile([P, PASSES, NH], I32, name="code_%s%d" % (name, g), align_bytes=64)
-            nc.sync.dma_start(t[:], words.rearrange("a p n i -> p a (n i)")[:, :, 4 * NH * g : 4 * NH * (g + 1)].bitcast(I32))
-            for a in range(PASSES):
-                codes[name, g, a] = t[:, a, :]
-
-        def load_packed_scales():
-            for w, (name, scales) in enumerate((("wb", wb_scales), ("wc", wc_scales))):
-                for q in range(4):
-                    nc.sync.dma_start(wbc_s[32 * q : 32 * q + 8, w, :], scales[:, 4 * q : 4 * q + 4, :].bitcast(I32))
-                for g in range(2):
-                    for a in range(PASSES):
-                        planes[name, g, a] = wbc_s[:, w, :].bitcast(U8)[4 * a : P, NH * g : NH * (g + 1)]
-
-        load_table(0)
-        load_float("wa", wa, 0)
-        load_table(1)
-        load_float("wo", wo, 0)
-        load_packed_scales()
-        load_packed("wb", wb_words, 0)
-        load_packed("wc", wc_words, 0)
-        nc.sync.dma_start(wgo_sb[:], wgo)
-        load_float("wa", wa, 1)
-        load_packed("wb", wb_words, 1)
-        load_packed("wc", wc_words, 1)
-        load_float("wo", wo, 1)
-
-        picked_w, picked_s = {}, {}
+        floats = {"wa": wa, "wo": wo}
+        words = {"wb": wb_words, "wc": wc_words}
+        scales = {"tab": tab_scales, "wb": wb_scales, "wc": wc_scales}
 
         def offsets(which, h):
             return lists[which][:, (JH // 16) * h : (JH // 16) * (h + 1)]
 
+        def zero(name):
+            if name.startswith("window"):
+                engines[OPT["zero_" + name]].memset(sb(name, [P, T], F32)[:], 0.0)
+            else:
+                engines[OPT["zero_" + name]].memset(sb(name, [P, (T if name == "s_tab" else N) // 4], I32)[:], 0)
+
+        def warm():
+            t = sb("warm", [P, 16], F32)
+            nc.vector.memset(t[:, 0:8], 0.0)
+            nc.scalar.activation(t[:, 8:16], t[:, 0:8], ACT.Sigmoid)
+
+        def identity():
+            make_identity(nc, sb("ident", [P, P], F32)[:])
+
+        def load_list(which):
+            nc.sync.dma_start(lists[which][:], offs if which == "src" else offs2)
+
+        def load_scales(name, q):
+            engines[OPT["q_" + name]].dma_start(tiles["s_" + name][32 * q : 32 * q + 8, :], scales[name][:, 4 * q : 4 * q + 4, :].bitcast(I32))
+
+        def load_table(a):
+            nc.sync.dma_start(sb("tab_w%d" % a, [P, T], I32)[:], tab_words[a].rearrange("p t i -> p (t i)").bitcast(I32))
+
+        parts = {}
+
+        def load_float(name, first, count, a):
+            t = sb("raw_%s%d%d" % (name, first, a), [P, 4, count * P], F32)
+            nc.sync.dma_start(t[:], floats[name][512 * a : 512 * (a + 1), P * first : P * (first + count)].rearrange("(p i) n -> p i n", i=4))
+            for i in range(count):
+                parts[name, first + i, a] = t[:, :, P * i : P * (i + 1)]
+
+        def load_packed(name, first, count):
+            t = sb("packed_%s%d" % (name, first), [P, PASSES, count * P], I32)
+            nc.sync.dma_start(t[:], words[name].rearrange("a p n i -> p a (n i)")[:, :, 4 * P * first : 4 * P * (first + count)].bitcast(I32))
+            for i in range(count):
+                for a in range(PASSES):
+                    parts[name, first + i, a] = t[:, a, P * i : P * (i + 1)]
+
+        def load_weight_column():
+            with nc.allow_non_contiguous_dma(reason="one weight to a partition"):
+                engines[OPT["q_wcol"]].dma_start(sb("w_col", [P, JH // P], F32)[:], wgo[0, 0:JH].rearrange("(b p) -> p b", p=P))
+
+        def load_weight_rows():
+            engines[OPT["q_wgo"]].dma_start(sb("wgo_sb", [P, J], F32)[:], wgo)
+
+        def spread_weights():
+            rows = bank("w_rows")
+            for b in range(JH // P):
+                nc.tensor.transpose(rows[:, P * b : P * (b + 1)], tiles["w_col"][:, b : b + 1].to_broadcast([P, P]), tiles["ident"][:])
+
+        def cast(name, nt, a):
+            t = sb("grp_%s%d" % (name, nt), [P, PASSES, P, 4], BF16)
+            source = parts[name, nt, a]
+            if OPT["cast_%s%d%d" % (name, nt, a)] == "G":
+                nc.gpsimd.tensor_scalar(t[:, a], source.rearrange("p i n -> p n i"), 1.0, 0.0, ALU.mult, ALU.add)
+            else:
+                nc.scalar.copy(t[:, a].rearrange("p (c e) i -> p c i e", e=4), source.rearrange("p i (c e) -> p c i e", e=4))
+
+        def quantise(name, nt):
+            c = sb("code_%s%d" % (name, nt), [P, PASSES * P], U32)
+            s = sb("plane_%s%d" % (name, nt), [P, PASSES * P], U8)
+            nc.vector.quantize_mx(c[:].bitcast(FP8X4), s[:], tiles["grp_%s%d" % (name, nt)][:].rearrange("p a n i -> p (a n i)"))
+
         def gather_scales(which, h):
-            t = keep.tile([P, JH], U8, name="ps_%s%d" % (which, h), align_bytes=64)
-            picked_s[which, h] = t
-            nc.vector.tensor_copy(t[:], tab_s[:].bitcast(U8).indirect(offsets(which, h)))
+            t = sb("ps_%s%d" % (which, h), [P, JH], U8)
+            nc.vector.tensor_copy(t[:], tiles["s_tab"][:].bitcast(U8).indirect(offsets(which, h)))
 
         def gather_words(which, a, h):
-            t = keep.tile([P, JH], U32, name="pw_%s%d%d" % (which, a, h), align_bytes=64)
-            picked_w[which, a, h] = t
-            nc.vector.tensor_copy(t[:], tab_w[a][:].bitcast(U32).indirect(offsets(which, h)))
+            t = sb("pw_%s%d%d" % (which, a, h), [P, JH], U32)
+            nc.vector.tensor_copy(t[:], tiles["tab_w%d" % a][:].bitcast(U32).indirect(offsets(which, h)))
 
-        for h in range(2):
-            for which in ("dst", "src"):
-                gather_scales(which, h)
-        cast("wa", 0)
-        cast("wo", 0)
-        for h in range(2):
-            for which in ("dst", "src"):
-                gather_words(which, 0, h)
-        quantise("wa", 0)
-        for which in ("dst", "src"):
-            gather_words(which, 1, 0)
-        quantise("wo", 0)
-        for which in ("dst", "src"):
-            gather_words(which, 1, 1)
-        cast("wa", 1)
-        cast("wo", 1)
+        def stationary(name, nt, a):
+            if name in floats:
+                cols = slice(P * a, P * (a + 1))
+                return tiles["code_%s%d" % (name, nt)][:, cols], tiles["plane_%s%d" % (name, nt)][:, cols]
+            return (
+                parts[name, nt, a],
+                tiles["s_" + name][:].bitcast(U8)[4 * a : P, P * nt : P * (nt + 1)],
+            )
 
-        def product(bank, terms, nt, h):
-            steps = [(name, which, a) for a in range(PASSES) for name, which in terms]
-            g, cols = nt // 2, slice(P * (nt % 2), P * (nt % 2 + 1))
+        terms = {"za": (("wa", "dst"), ("wb", "src")), "ms": (("wc", "src"),), "ow": (("wo", "dst"),)}
+
+        def product(kind, u):
+            nt, h = UNITS[u]
+            acc = bank("%s%d" % (kind, u))
+            steps = [(name, which, a) for a in range(PASSES) for name, which in terms[kind]]
             for i, (name, which, a) in enumerate(steps):
+                codes, plane = stationary(name, nt, a)
                 nc.tensor.matmul_mx(
-                    bank[:],
-                    lhsT=codes[name, g, a][:, cols].bitcast(FP8X4),
-                    lhsT_scale=planes[name, g, a][:, cols],
-                    rhs=picked_w[which, a, h][:].bitcast(FP8X4),
-                    rhs_scale=picked_s[which, h][4 * a : P, :],
+                    acc[:],
+                    lhsT=codes.bitcast(FP8X4),
+                    lhsT_scale=plane,
+                    rhs=tiles["pw_%s%d%d" % (which, a, h)][:].bitcast(FP8X4),
+                    rhs_scale=tiles["ps_%s%d" % (which, h)][4 * a : P, :],
                     start=(i == 0),
                     stop=(i == len(steps) - 1),
                 )
 
-        units = [(0, 0), (1, 0), (0, 1), (1, 1), (2, 0), (2, 1), (3, 0), (3, 1)]
-        state = {}
+        def row(kind, u):
+            return sb("%s%d" % (kind, u), [P, JH], F32)
 
-        def multiply(u):
-            nt, h = units[u]
-            za = psum.tile([P, JH], F32, name="za", tag="za", bufs=2)
-            ms = psum.tile([P, JH], F32, name="ms", tag="ms", bufs=3)
-            ow = psum.tile([P, JH], F32, name="ow", tag="ow", bufs=3)
-            product(za, (("wa", "dst"), ("wb", "src")), nt, h)
-            product(ms, (("wc", "src"),), nt, h)
-            product(ow, (("wo", "dst"),), nt, h)
-            eta = work.tile([P, JH], F32, name="eta")
-            nc.scalar.activation(eta[:], za[:], ACT.Sigmoid)
-            state[u] = (eta, ms, ow)
+        def evacuate(kind, u):
+            if kind == "za":
+                nc.scalar.activation(row("eta", u)[:], tiles["za%d" % u][:], ACT.Sigmoid)
+            elif OPT[("gate%d" if kind == "ms" else "add%d") % u] == "G":
+                nc.scalar.copy(row(kind + "_sb", u)[:], tiles["%s%d" % (kind, u)][:])
 
         def gate(u):
-            eta, ms, ow = state[u]
-            msg = work.tile([P, JH], F32, name="msg")
-            nc.vector.tensor_tensor(msg[:], ms[:], eta[:], ALU.mult)
-            state[u] = (msg, ow)
+            e = OPT["gate%d" % u]
+            engines[e].tensor_tensor(row("msg", u)[:], tiles[("ms_sb%d" if e == "G" else "ms%d") % u][:], tiles["eta%d" % u][:], ALU.mult)
 
         def add(u):
-            msg, ow = state[u]
-            y = work.tile([P, JH], F32, name="y")
-            nc.vector.tensor_tensor(y[:], ow[:], msg[:], ALU.add)
-            state[u] = y
+            e = OPT["add%d" % u]
+            engines[e].tensor_tensor(row("y", u)[:], tiles[("ow_sb%d" if e == "G" else "ow%d") % u][:], tiles["msg%d" % u][:], ALU.add)
+
+        def rectify(u):
+            if OPT["weigh%d" % u] != "V":
+                nc.scalar.activation(row("pos", u)[:], tiles["y%d" % u][:], ACT.Relu)
 
         def weigh(u):
-            h = units[u][1]
-            r = work.tile([P, JH], F32, name="r")
-            nc.vector.scalar_tensor_tensor(r[:], state[u][:], 0.0, wgo_sb[:, JH * h : JH * (h + 1)], ALU.max, ALU.mult)
-            state[u] = r
+            h = UNITS[u][1]
+            if OPT["weigh%d" % u] == "V":
+                nc.vector.scalar_tensor_tensor(row("r", u)[:], tiles["y%d" % u][:], 0.0, tiles["w_rows"][:], ALU.max, ALU.mult)
+            elif OPT["weigh%d" % u] == "G":
+                nc.gpsimd.tensor_tensor(row("r", u)[:], tiles["pos%d" % u][:], tiles["wgo_sb"][:, JH * h : JH * (h + 1)], ALU.mult)
 
         def scatter(u):
-            nt, h = units[u]
-            win = windows[nt % 3]
-            nc.vector.tensor_copy(win[:].indirect(offsets("dst", h)), state[u][:])
+            nt, h = UNITS[u]
+            window = tiles["window%d" % nt]
+            if OPT["weigh%d" % u] == "F":
+                nc.vector.tensor_tensor(window[:].indirect(offsets("dst", h)), tiles["pos%d" % u][:], tiles["wgo_sb"][:, JH * h : JH * (h + 1)], ALU.mult)
+            else:
+                nc.vector.tensor_copy(window[:].indirect(offsets("dst", h)), tiles["r%d" % u][:])
             if h == 1:
-                nc.sync.dma_start(out[P * nt : P * (nt + 1), :], win[:])
+                nc.sync.dma_start(out[P * nt : P * (nt + 1), :], window[:])
 
-        multiply(0)
-        multiply(1)
-        gate(0)
-        for u in range(len(units)):
-            if u + 2 < len(units):
-                if u == 2:
-                    quantise("wa", 1)
-                    quantise("wo", 1)
-                multiply(u + 2)
-            add(u)
-            if u + 1 < len(units):
-                gate(u + 1)
-            weigh(u)
-            if u > 0:
-                scatter(u - 1)
-        scatter(len(units) - 1)
+        actions = {
+            "zero": zero, "warm": warm, "identity": identity, "load_list": load_list, "load_scales": load_scales,
+            "load_table": load_table, "load_float": load_float, "load_packed": load_packed,
+            "load_weight_column": load_weight_column, "load_weight_rows": load_weight_rows, "spread_weights": spread_weights,
+            "cast": cast, "quantise": quantise, "gather_scales": gather_scales, "gather_words": gather_words,
+            "product": product, "evacuate": evacuate, "gate": gate, "add": add, "rectify": rectify, "weigh": weigh, "scatter": scatter,
+        }
+        for step in STEPS:
+            actions[step[0]](*step[1:])

@@ -21,59 +21,59 @@ PASSES = 2
 JH = 512
 UNITS = ((0, 0), (1, 0), (0, 1), (1, 1), (2, 0), (2, 1), (3, 0), (3, 1))
 
-STEPS = (('load_float', 'wa', 0, 2, 0), ('zero', 's_tab'), ('zero', 's_wb'), ('load_list', 'dst'), ('zero', 's_wc'), ('load_scales', 'tab', 0),
- ('load_scales', 'tab', 3), ('load_scales', 'wb', 2), ('load_scales', 'tab', 2), ('load_scales', 'tab', 1), ('load_table', 0), ('cast', 'wa', 1, 0),
- ('load_list', 'src'), ('load_scales', 'wc', 3), ('load_scales', 'wc', 2), ('load_float', 'wa', 0, 2, 1), ('cast', 'wa', 1, 1),
- ('load_scales', 'wb', 0), ('gather_words', 'dst', 0, 0), ('load_scales', 'wc', 1), ('load_float', 'wo', 0, 2, 0), ('load_table', 1),
- ('gather_words', 'src', 1, 0), ('cast', 'wa', 0, 1), ('gather_words', 'dst', 1, 0), ('gather_scales', 'src', 1), ('zero', 'window3'),
- ('load_float', 'wa', 2, 2, 0), ('warm',), ('identity',), ('gather_scales', 'src', 0), ('gather_words', 'src', 0, 0), ('load_scales', 'wb', 1),
- ('load_scales', 'wb', 3), ('load_weight_column',), ('load_packed', 'wb', 0, 2), ('cast', 'wa', 0, 0), ('quantise', 'wa', 0),
- ('gather_scales', 'dst', 1), ('gather_words', 'src', 0, 1), ('cast', 'wa', 2, 0), ('load_float', 'wo', 0, 2, 1), ('load_packed', 'wc', 0, 2),
- ('load_scales', 'wc', 0), ('gather_words', 'src', 1, 1), ('gather_scales', 'dst', 0), ('load_float', 'wa', 2, 2, 1), ('load_float', 'wo', 2, 2, 0),
- ('cast', 'wo', 1, 0), ('cast', 'wo', 0, 0), ('cast', 'wo', 0, 1), ('cast', 'wo', 1, 1), ('quantise', 'wa', 1), ('gather_words', 'dst', 0, 1),
- ('quantise', 'wo', 0), ('load_packed', 'wc', 2, 2), ('product', 'za', 0), ('evacuate', 'za', 0), ('product', 'ms', 2), ('cast', 'wa', 2, 1),
- ('product', 'ms', 0), ('evacuate', 'ms', 0), ('quantise', 'wo', 1), ('gate', 0), ('product', 'za', 1), ('product', 'ms', 1), ('product', 'ow', 0),
- ('evacuate', 'ms', 1), ('zero', 'window0'), ('evacuate', 'ms', 2), ('load_weight_rows',), ('evacuate', 'ow', 0), ('gather_words', 'dst', 1, 1),
- ('add', 0), ('product', 'ow', 2), ('evacuate', 'za', 1), ('cast', 'wa', 3, 1), ('product', 'ow', 1), ('gate', 1), ('load_float', 'wo', 2, 2, 1),
- ('evacuate', 'ow', 1), ('add', 1), ('load_packed', 'wb', 2, 2), ('spread_weights',), ('product', 'za', 2), ('evacuate', 'za', 2),
- ('zero', 'window2'), ('zero', 'window1'), ('evacuate', 'ow', 2), ('gate', 2), ('rectify', 1), ('cast', 'wa', 3, 0), ('product', 'ms', 3),
- ('cast', 'wo', 2, 0), ('quantise', 'wa', 2), ('cast', 'wo', 3, 1), ('quantise', 'wa', 3), ('rectify', 0), ('product', 'ms', 6), ('product', 'za', 3),
- ('weigh', 0), ('scatter', 0), ('evacuate', 'ms', 3), ('weigh', 1), ('product', 'ms', 4), ('evacuate', 'za', 3), ('evacuate', 'ms', 4),
- ('cast', 'wo', 3, 0), ('product', 'za', 4), ('evacuate', 'za', 4), ('product', 'ow', 3), ('cast', 'wo', 2, 1), ('add', 2), ('rectify', 2),
- ('product', 'za', 6), ('scatter', 1), ('gate', 3), ('gate', 4), ('weigh', 2), ('evacuate', 'ow', 3), ('quantise', 'wo', 2), ('product', 'za', 5),
- ('quantise', 'wo', 3), ('scatter', 2), ('product', 'ow', 6), ('evacuate', 'za', 6), ('evacuate', 'ms', 6), ('product', 'ow', 4), ('gate', 6),
- ('evacuate', 'ow', 4), ('product', 'ms', 7), ('evacuate', 'ow', 6), ('evacuate', 'ms', 7), ('product', 'ms', 5), ('add', 4), ('product', 'ow', 5),
- ('evacuate', 'za', 5), ('add', 6), ('product', 'ow', 7), ('product', 'za', 7), ('rectify', 4), ('evacuate', 'ow', 5), ('add', 3), ('rectify', 6),
- ('evacuate', 'ms', 5), ('gate', 5), ('add', 5), ('weigh', 4), ('rectify', 5), ('rectify', 3), ('evacuate', 'za', 7), ('evacuate', 'ow', 7),
- ('scatter', 4), ('gate', 7), ('weigh', 3), ('weigh', 5), ('add', 7), ('scatter', 3), ('rectify', 7), ('scatter', 5), ('weigh', 7), ('weigh', 6),
- ('scatter', 6), ('scatter', 7))
-CHAINS = (('eta1', 'plane_wa2'), ('code_wa3', 'ow_sb5'), ('eta6', 'ms_sb7'), ('grp_wa1', 'raw_wo21'), ('grp_wa3', 'y2'), ('raw_wa01', 'grp_wo1'),
- ('raw_wa21', 'r0'), ('eta3', 'ow_sb3'), ('ms_sb2', 'msg3'), ('grp_wa0', 'pw_src11'))
+STEPS = (('identity',), ('zero', 's_tab'), ('load_float', 'wa', 0, 2, 0), ('load_list', 'dst'), ('zero', 's_wc'), ('load_scales', 'tab', 3),
+ ('load_scales', 'tab', 1), ('load_scales', 'tab', 2), ('load_scales', 'tab', 0), ('load_list', 'src'), ('cast', 'wa', 0, 0), ('load_table', 0),
+ ('load_weight_column',), ('zero', 's_wb'), ('gather_scales', 'src', 1), ('load_scales', 'wb', 3), ('load_scales', 'wc', 2), ('load_scales', 'wc', 3),
+ ('cast', 'wa', 1, 0), ('load_float', 'wa', 0, 2, 1), ('load_scales', 'wb', 1), ('gather_words', 'src', 0, 0), ('load_table', 1),
+ ('load_scales', 'wc', 1), ('gather_scales', 'dst', 0), ('gather_words', 'dst', 1, 0), ('warm',), ('gather_words', 'src', 1, 0), ('cast', 'wa', 0, 1),
+ ('load_float', 'wa', 2, 2, 0), ('load_scales', 'wb', 2), ('gather_words', 'src', 0, 1), ('load_packed', 'wb', 0, 2), ('load_float', 'wo', 0, 2, 0),
+ ('load_scales', 'wb', 0), ('gather_words', 'src', 1, 1), ('gather_words', 'dst', 0, 0), ('quantise', 'wa', 0), ('cast', 'wo', 1, 0),
+ ('load_float', 'wo', 0, 2, 1), ('cast', 'wo', 1, 1), ('load_scales', 'wc', 0), ('gather_scales', 'dst', 1), ('gather_scales', 'src', 0),
+ ('cast', 'wa', 1, 1), ('cast', 'wo', 0, 0), ('load_packed', 'wc', 0, 2), ('zero', 'window3'), ('quantise', 'wa', 1), ('product', 'ms', 2),
+ ('cast', 'wo', 0, 1), ('product', 'ms', 0), ('evacuate', 'ms', 0), ('quantise', 'wo', 1), ('product', 'za', 0), ('quantise', 'wo', 0),
+ ('evacuate', 'za', 0), ('spread_weights',), ('zero', 'window0'), ('product', 'za', 1), ('gather_words', 'dst', 1, 1), ('product', 'ow', 0),
+ ('gather_words', 'dst', 0, 1), ('cast', 'wa', 3, 0), ('load_packed', 'wb', 2, 2), ('evacuate', 'za', 1), ('cast', 'wa', 2, 0), ('evacuate', 'ms', 1),
+ ('evacuate', 'ow', 0), ('product', 'ms', 1), ('load_float', 'wo', 2, 2, 0), ('load_packed', 'wc', 2, 2), ('gate', 1), ('product', 'ow', 1),
+ ('evacuate', 'ow', 1), ('load_float', 'wa', 2, 2, 1), ('cast', 'wa', 3, 1), ('load_float', 'wo', 2, 2, 1), ('add', 1), ('gate', 0),
+ ('evacuate', 'ms', 2), ('product', 'ms', 4), ('product', 'za', 2), ('cast', 'wa', 2, 1), ('cast', 'wo', 3, 1), ('quantise', 'wa', 2),
+ ('product', 'ow', 2), ('add', 0), ('product', 'za', 4), ('product', 'ms', 6), ('evacuate', 'za', 2), ('evacuate', 'ow', 2), ('evacuate', 'ms', 4),
+ ('rectify', 0), ('product', 'ms', 3), ('cast', 'wo', 3, 0), ('weigh', 0), ('evacuate', 'ms', 6), ('quantise', 'wa', 3), ('gate', 2),
+ ('cast', 'wo', 2, 1), ('zero', 'window1'), ('quantise', 'wo', 3), ('rectify', 1), ('evacuate', 'ms', 3), ('product', 'za', 6), ('product', 'ow', 3),
+ ('add', 2), ('weigh', 1), ('product', 'za', 3), ('scatter', 0), ('rectify', 2), ('evacuate', 'za', 3), ('evacuate', 'ow', 3), ('evacuate', 'za', 6),
+ ('load_weight_rows',), ('evacuate', 'za', 4), ('cast', 'wo', 2, 0), ('quantise', 'wo', 2), ('scatter', 1), ('gate', 3), ('gate', 4), ('gate', 6),
+ ('product', 'ow', 6), ('evacuate', 'ow', 6), ('product', 'ow', 4), ('evacuate', 'ow', 4), ('add', 6), ('product', 'ow', 7), ('product', 'za', 5),
+ ('product', 'za', 7), ('add', 3), ('product', 'ms', 5), ('rectify', 3), ('weigh', 3), ('evacuate', 'za', 7), ('zero', 'window2'), ('weigh', 2),
+ ('evacuate', 'za', 5), ('product', 'ow', 5), ('product', 'ms', 7), ('add', 4), ('rectify', 4), ('evacuate', 'ms', 5), ('weigh', 4), ('scatter', 2),
+ ('evacuate', 'ow', 7), ('weigh', 5), ('evacuate', 'ms', 7), ('scatter', 3), ('scatter', 4), ('gate', 5), ('gate', 7), ('rectify', 6), ('weigh', 6),
+ ('add', 7), ('rectify', 7), ('evacuate', 'ow', 5), ('add', 5), ('weigh', 7), ('rectify', 5), ('scatter', 6), ('scatter', 5), ('scatter', 7))
+CHAINS = (('tab_w1', 'window1'), ('grp_wo1', 'pw_dst11'), ('r0', 'window2'), ('msg1', 'y2'), ('raw_wa20', 'y7'), ('code_wo0', 'pos2'), ('grp_wa1', 'pw_dst01'),
+ ('plane_wa0', 'msg2', 'msg4'), ('eta7', 'pos7'), ('plane_wo0', 'ms_sb3'), ('code_wo3', 'pos3'), ('grp_wo0', 'plane_wa3'), ('y4', 'msg5'),
+ ('ident', 'grp_wa3'))
 BANKS = {'ms0': 0,
- 'ms1': 5,
- 'ms2': 4,
+ 'ms1': 4,
+ 'ms2': 6,
  'ms3': 6,
- 'ms4': 4,
- 'ms5': 5,
- 'ms6': 1,
+ 'ms4': 3,
+ 'ms5': 6,
+ 'ms6': 2,
  'ms7': 2,
- 'ow0': 2,
- 'ow1': 4,
- 'ow2': 1,
- 'ow3': 4,
- 'ow4': 0,
- 'ow5': 0,
- 'ow6': 5,
- 'ow7': 4,
+ 'ow0': 1,
+ 'ow1': 2,
+ 'ow2': 5,
+ 'ow3': 5,
+ 'ow4': 4,
+ 'ow5': 3,
+ 'ow6': 1,
+ 'ow7': 5,
  'w_rows': 7,
- 'za0': 1,
- 'za1': 6,
- 'za2': 0,
- 'za3': 0,
- 'za4': 2,
+ 'za0': 5,
+ 'za1': 3,
+ 'za2': 4,
+ 'za3': 1,
+ 'za4': 0,
  'za5': 3,
- 'za6': 0,
- 'za7': 6}
+ 'za6': 4,
+ 'za7': 0}
 OPT = {'add0': 'V',
  'add1': 'V',
  'add2': 'G',
@@ -89,9 +89,9 @@ OPT = {'add0': 'V',
  'cast_wa20': 'S',
  'cast_wa21': 'S',
  'cast_wa30': 'S',
- 'cast_wa31': 'G',
- 'cast_wo00': 'G',
- 'cast_wo01': 'G',
+ 'cast_wa31': 'S',
+ 'cast_wo00': 'S',
+ 'cast_wo01': 'S',
  'cast_wo10': 'S',
  'cast_wo11': 'S',
  'cast_wo20': 'S',
@@ -102,9 +102,9 @@ OPT = {'add0': 'V',
  'gate1': 'V',
  'gate2': 'G',
  'gate3': 'G',
- 'gate4': 'G',
+ 'gate4': 'V',
  'gate5': 'G',
- 'gate6': 'G',
+ 'gate6': 'V',
  'gate7': 'G',
  'q_tab': 'SP',
  'q_wb': 'SP',
@@ -116,16 +116,17 @@ OPT = {'add0': 'V',
  'weigh2': 'G',
  'weigh3': 'G',
  'weigh4': 'V',
- 'weigh5': 'G',
- 'weigh6': 'V',
+ 'weigh5': 'F',
+ 'weigh6': 'G',
  'weigh7': 'F',
+ 'windows': 3,
  'zero_s_tab': 'V',
  'zero_s_wb': 'G',
  'zero_s_wc': 'V',
  'zero_window0': 'V',
  'zero_window1': 'G',
  'zero_window2': 'G',
- 'zero_window3': 'V'}
+ 'zero_window3': 'G'}
 
 
 def tile_list_rgg_ownrelu_kernel(
@@ -158,7 +159,8 @@ def tile_list_rgg_ownrelu_kernel(
 
         def zero(name):
             if name.startswith("window"):
-                engines[OPT["zero_" + name]].memset(sb(name, [P, T], F32)[:], 0.0)
+                if int(name[-1]) < OPT["windows"]:
+                    engines[OPT["zero_" + name]].memset(sb(name, [P, T], F32)[:].bitcast(I32), 0)
             else:
                 engines[OPT["zero_" + name]].memset(sb(name, [P, (T if name == "s_tab" else N) // 4], I32)[:], 0)
 
@@ -284,7 +286,7 @@ def tile_list_rgg_ownrelu_kernel(
 
         def scatter(u):
             nt, h = UNITS[u]
-            window = tiles["window%d" % nt]
+            window = tiles["window%d" % (nt % OPT["windows"])]
             if OPT["weigh%d" % u] == "F":
                 nc.vector.tensor_tensor(window[:].indirect(offsets("dst", h)), tiles["pos%d" % u][:], tiles["wgo_sb"][:, JH * h : JH * (h + 1)], ALU.mult)
             else:

@@ -17,289 +17,293 @@ ACT = mybir.ActivationFunctionType
 ALU = mybir.AluOpType
 
 P = 128
-PASSES = 2
-JH = 512
-UNITS = ((0, 0), (1, 0), (0, 1), (1, 1), (2, 0), (2, 1), (3, 0), (3, 1))
+PACK = 4
+K_PASS = P * PACK
+PASSES = K // K_PASS
+JH = J // 2
+NH = N // 2
+BANK = 512
+PER_COLUMN = 16
 
-STEPS = (('identity',), ('zero', 's_tab'), ('load_float', 'wa', 0, 2, 0), ('load_list', 'dst'), ('zero', 's_wc'), ('load_scales', 'tab', 3),
- ('load_scales', 'tab', 1), ('load_scales', 'tab', 2), ('load_scales', 'tab', 0), ('load_list', 'src'), ('cast', 'wa', 0, 0), ('load_table', 0),
- ('load_weight_column',), ('zero', 's_wb'), ('gather_scales', 'src', 1), ('load_scales', 'wb', 3), ('load_scales', 'wc', 2), ('load_scales', 'wc', 3),
- ('cast', 'wa', 1, 0), ('load_float', 'wa', 0, 2, 1), ('load_scales', 'wb', 1), ('gather_words', 'src', 0, 0), ('load_table', 1),
- ('load_scales', 'wc', 1), ('gather_scales', 'dst', 0), ('gather_words', 'dst', 1, 0), ('warm',), ('gather_words', 'src', 1, 0), ('cast', 'wa', 0, 1),
- ('load_float', 'wa', 2, 2, 0), ('load_scales', 'wb', 2), ('gather_words', 'src', 0, 1), ('load_packed', 'wb', 0, 2), ('load_float', 'wo', 0, 2, 0),
- ('load_scales', 'wb', 0), ('gather_words', 'src', 1, 1), ('gather_words', 'dst', 0, 0), ('quantise', 'wa', 0), ('cast', 'wo', 1, 0),
- ('load_float', 'wo', 0, 2, 1), ('cast', 'wo', 1, 1), ('load_scales', 'wc', 0), ('gather_scales', 'dst', 1), ('gather_scales', 'src', 0),
- ('cast', 'wa', 1, 1), ('cast', 'wo', 0, 0), ('load_packed', 'wc', 0, 2), ('zero', 'window3'), ('quantise', 'wa', 1), ('product', 'ms', 2),
- ('cast', 'wo', 0, 1), ('product', 'ms', 0), ('evacuate', 'ms', 0), ('quantise', 'wo', 1), ('product', 'za', 0), ('quantise', 'wo', 0),
- ('evacuate', 'za', 0), ('spread_weights',), ('zero', 'window0'), ('product', 'za', 1), ('gather_words', 'dst', 1, 1), ('product', 'ow', 0),
- ('gather_words', 'dst', 0, 1), ('cast', 'wa', 3, 0), ('load_packed', 'wb', 2, 2), ('evacuate', 'za', 1), ('cast', 'wa', 2, 0), ('evacuate', 'ms', 1),
- ('evacuate', 'ow', 0), ('product', 'ms', 1), ('load_float', 'wo', 2, 2, 0), ('load_packed', 'wc', 2, 2), ('gate', 1), ('product', 'ow', 1),
- ('evacuate', 'ow', 1), ('load_float', 'wa', 2, 2, 1), ('cast', 'wa', 3, 1), ('load_float', 'wo', 2, 2, 1), ('add', 1), ('gate', 0),
- ('evacuate', 'ms', 2), ('product', 'ms', 4), ('product', 'za', 2), ('cast', 'wa', 2, 1), ('cast', 'wo', 3, 1), ('quantise', 'wa', 2),
- ('product', 'ow', 2), ('add', 0), ('product', 'za', 4), ('product', 'ms', 6), ('evacuate', 'za', 2), ('evacuate', 'ow', 2), ('evacuate', 'ms', 4),
- ('rectify', 0), ('product', 'ms', 3), ('cast', 'wo', 3, 0), ('weigh', 0), ('evacuate', 'ms', 6), ('quantise', 'wa', 3), ('gate', 2),
- ('cast', 'wo', 2, 1), ('zero', 'window1'), ('quantise', 'wo', 3), ('rectify', 1), ('evacuate', 'ms', 3), ('product', 'za', 6), ('product', 'ow', 3),
- ('add', 2), ('weigh', 1), ('product', 'za', 3), ('scatter', 0), ('rectify', 2), ('evacuate', 'za', 3), ('evacuate', 'ow', 3), ('evacuate', 'za', 6),
- ('load_weight_rows',), ('evacuate', 'za', 4), ('cast', 'wo', 2, 0), ('quantise', 'wo', 2), ('scatter', 1), ('gate', 3), ('gate', 4), ('gate', 6),
- ('product', 'ow', 6), ('evacuate', 'ow', 6), ('product', 'ow', 4), ('evacuate', 'ow', 4), ('add', 6), ('product', 'ow', 7), ('product', 'za', 5),
- ('product', 'za', 7), ('add', 3), ('product', 'ms', 5), ('rectify', 3), ('weigh', 3), ('evacuate', 'za', 7), ('zero', 'window2'), ('weigh', 2),
- ('evacuate', 'za', 5), ('product', 'ow', 5), ('product', 'ms', 7), ('add', 4), ('rectify', 4), ('evacuate', 'ms', 5), ('weigh', 4), ('scatter', 2),
- ('evacuate', 'ow', 7), ('weigh', 5), ('evacuate', 'ms', 7), ('scatter', 3), ('scatter', 4), ('gate', 5), ('gate', 7), ('rectify', 6), ('weigh', 6),
- ('add', 7), ('rectify', 7), ('evacuate', 'ow', 5), ('add', 5), ('weigh', 7), ('rectify', 5), ('scatter', 6), ('scatter', 5), ('scatter', 7))
-CHAINS = (('tab_w1', 'window1'), ('grp_wo1', 'pw_dst11'), ('r0', 'window2'), ('msg1', 'y2'), ('raw_wa20', 'y7'), ('code_wo0', 'pos2'), ('grp_wa1', 'pw_dst01'),
- ('plane_wa0', 'msg2', 'msg4'), ('eta7', 'pos7'), ('plane_wo0', 'ms_sb3'), ('code_wo3', 'pos3'), ('grp_wo0', 'plane_wa3'), ('y4', 'msg5'),
- ('ident', 'grp_wa3'))
-BANKS = {'ms0': 0,
- 'ms1': 4,
- 'ms2': 6,
- 'ms3': 6,
- 'ms4': 3,
- 'ms5': 6,
- 'ms6': 2,
- 'ms7': 2,
- 'ow0': 1,
- 'ow1': 2,
- 'ow2': 5,
- 'ow3': 5,
- 'ow4': 4,
- 'ow5': 3,
- 'ow6': 1,
- 'ow7': 5,
- 'w_rows': 7,
- 'za0': 5,
- 'za1': 3,
- 'za2': 4,
- 'za3': 1,
- 'za4': 0,
- 'za5': 3,
- 'za6': 4,
- 'za7': 0}
-OPT = {'add0': 'V',
- 'add1': 'V',
- 'add2': 'G',
- 'add3': 'G',
- 'add4': 'V',
- 'add5': 'G',
- 'add6': 'G',
- 'add7': 'G',
- 'cast_wa00': 'S',
- 'cast_wa01': 'S',
- 'cast_wa10': 'S',
- 'cast_wa11': 'S',
- 'cast_wa20': 'S',
- 'cast_wa21': 'S',
- 'cast_wa30': 'S',
- 'cast_wa31': 'S',
- 'cast_wo00': 'S',
- 'cast_wo01': 'S',
- 'cast_wo10': 'S',
- 'cast_wo11': 'S',
- 'cast_wo20': 'S',
- 'cast_wo21': 'S',
- 'cast_wo30': 'S',
- 'cast_wo31': 'S',
- 'gate0': 'V',
- 'gate1': 'V',
- 'gate2': 'G',
- 'gate3': 'G',
- 'gate4': 'V',
- 'gate5': 'G',
- 'gate6': 'V',
- 'gate7': 'G',
- 'q_tab': 'SP',
- 'q_wb': 'SP',
- 'q_wc': 'SP',
- 'q_wcol': 'SP',
- 'q_wgo': 'SP',
- 'weigh0': 'V',
- 'weigh1': 'V',
- 'weigh2': 'G',
- 'weigh3': 'G',
- 'weigh4': 'V',
- 'weigh5': 'F',
- 'weigh6': 'G',
- 'weigh7': 'F',
- 'windows': 3,
- 'zero_s_tab': 'V',
- 'zero_s_wb': 'G',
- 'zero_s_wc': 'V',
- 'zero_window0': 'V',
- 'zero_window1': 'G',
- 'zero_window2': 'G',
- 'zero_window3': 'G'}
+UNITS = tuple((g, h, pair) for g in range(2) for h in range(2) for pair in range(2))
+PIECES = tuple((2 * g + t, h) for g in range(2) for h in range(2) for t in range(2))
+
+BANKS = {"za": (0, 2), "ms": (2, 3), "ow": (5, 2), "y": (7, 1)}
+
+WINDOWS = 2
+
+TAKES_BYTES_OF = {
+    "pw_src11": "raw_wo01",
+    "pw_dst01": "eta0",
+    "grp_wo10": "msg1",
+    "grp_wo11": "plane_wo01",
+}
 
 
 def tile_list_rgg_ownrelu_kernel(
     tc, tab_words, tab_scales, wa, wb_words, wb_scales, wc_words, wc_scales, wo, wgo, offs, offs2, out
 ):
     nc = tc.nc
-    engines = {"V": nc.vector, "G": nc.gpsimd, "S": nc.scalar, "SP": nc.sync}
     with ExitStack() as ctx:
         keep = ctx.enter_context(tc.tile_pool(name="keep", bufs=1))
         psum = ctx.enter_context(tc.psum_pool(name="psum", bufs=1))
-        slot_of = {name: chain[0] for chain in CHAINS for name in chain}
         tiles = {}
+        banks_taken = {kind: 0 for kind in BANKS}
 
-        def sb(name, shape, dtype):
-            if name not in tiles:
-                tiles[name] = keep.tile(shape, dtype, name=name, tag=slot_of.get(name, name), align_bytes=64)
+        def sbuf(name, shape, dtype):
+            tiles[name] = keep.tile(shape, dtype, name=name, tag=TAKES_BYTES_OF.get(name, name), align_bytes=64)
             return tiles[name]
 
-        def bank(name):
-            tiles[name] = psum.tile([P, JH], F32, name=name, tag="bank%d" % BANKS[name])
+        def next_bank(kind, index):
+            first, count = BANKS[kind]
+            name = "%s%d" % (kind, index)
+            tiles[name] = psum.tile([P, BANK], F32, name=name, tag="bank%d" % (first + banks_taken[kind] % count))
+            banks_taken[kind] += 1
             return tiles[name]
 
-        lists = {"src": keep.tile([P, J // 16], U16, name="list_src"), "dst": keep.tile([P, J // 16], U16, name="list_dst")}
-        floats = {"wa": wa, "wo": wo}
-        words = {"wb": wb_words, "wc": wc_words}
-        scales = {"tab": tab_scales, "wb": wb_scales, "wc": wc_scales}
+        lists = {
+            "src": keep.tile([P, J // PER_COLUMN], U16, name="list_src"),
+            "dst": keep.tile([P, J // PER_COLUMN], U16, name="list_dst"),
+        }
+        float_weights = {"wa": wa, "wo": wo}
+        packed_weights = {"wb": wb_words, "wc": wc_words}
+        scale_rows = {"tab": tab_scales, "wb": wb_scales, "wc": wc_scales}
 
         def offsets(which, h):
-            return lists[which][:, (JH // 16) * h : (JH // 16) * (h + 1)]
+            return lists[which][:, (JH // PER_COLUMN) * h : (JH // PER_COLUMN) * (h + 1)]
 
-        def zero(name):
-            if name.startswith("window"):
-                if int(name[-1]) < OPT["windows"]:
-                    engines[OPT["zero_" + name]].memset(sb(name, [P, T], F32)[:].bitcast(I32), 0)
-            else:
-                engines[OPT["zero_" + name]].memset(sb(name, [P, (T if name == "s_tab" else N) // 4], I32)[:], 0)
+        nc.vector.memset(sbuf("s_tab", [P, T // 4], I32)[:], 0)
+        nc.gpsimd.memset(sbuf("window0", [P, T], F32)[:].bitcast(I32), 0)
+        make_identity(nc, sbuf("ident", [P, P], F32)[:])
+        nc.gpsimd.memset(sbuf("s_wc", [P, N // 4], I32)[:], 0)
+        nc.gpsimd.memset(sbuf("s_wb", [P, N // 4], I32)[:], 0)
+        nc.gpsimd.memset(sbuf("window1", [P, T], F32)[:].bitcast(I32), 0)
 
-        def warm():
-            t = sb("warm", [P, 16], F32)
-            nc.vector.memset(t[:, 0:8], 0.0)
-            nc.scalar.activation(t[:, 8:16], t[:, 0:8], ACT.Sigmoid)
-
-        def identity():
-            make_identity(nc, sb("ident", [P, P], F32)[:])
-
-        def load_list(which):
-            nc.sync.dma_start(lists[which][:], offs if which == "src" else offs2)
-
-        def load_scales(name, q):
-            engines[OPT["q_" + name]].dma_start(tiles["s_" + name][32 * q : 32 * q + 8, :], scales[name][:, 4 * q : 4 * q + 4, :].bitcast(I32))
+        def load_scales(name, quadrants):
+            for quadrant in quadrants:
+                nc.sync.dma_start(
+                    tiles["s_" + name][32 * quadrant : 32 * quadrant + 4 * PASSES, :],
+                    scale_rows[name][:, 4 * quadrant : 4 * quadrant + 4, :].bitcast(I32),
+                )
 
         def load_table(a):
-            nc.sync.dma_start(sb("tab_w%d" % a, [P, T], I32)[:], tab_words[a].rearrange("p t i -> p (t i)").bitcast(I32))
+            nc.sync.dma_start(sbuf("tab_w%d" % a, [P, T], I32)[:], tab_words[a].rearrange("p t i -> p (t i)").bitcast(I32))
 
-        parts = {}
+        def load_float(name, g, a):
+            rows = float_weights[name][K_PASS * a : K_PASS * (a + 1), NH * g : NH * (g + 1)]
+            nc.sync.dma_start(sbuf("raw_%s%d%d" % (name, g, a), [P, PACK, NH], F32)[:], rows.rearrange("(p i) n -> p i n", i=PACK))
 
-        def load_float(name, first, count, a):
-            t = sb("raw_%s%d%d" % (name, first, a), [P, 4, count * P], F32)
-            nc.sync.dma_start(t[:], floats[name][512 * a : 512 * (a + 1), P * first : P * (first + count)].rearrange("(p i) n -> p i n", i=4))
-            for i in range(count):
-                parts[name, first + i, a] = t[:, :, P * i : P * (i + 1)]
+        def load_packed(name, g):
+            codes = packed_weights[name].rearrange("a p n i -> p a (n i)")[:, :, PACK * NH * g : PACK * NH * (g + 1)]
+            nc.sync.dma_start(sbuf("packed_%s%d" % (name, g), [P, PASSES, NH], I32)[:], codes.bitcast(I32))
 
-        def load_packed(name, first, count):
-            t = sb("packed_%s%d" % (name, first), [P, PASSES, count * P], I32)
-            nc.sync.dma_start(t[:], words[name].rearrange("a p n i -> p a (n i)")[:, :, 4 * P * first : 4 * P * (first + count)].bitcast(I32))
-            for i in range(count):
-                for a in range(PASSES):
-                    parts[name, first + i, a] = t[:, a, P * i : P * (i + 1)]
+        def load_edge_weights(h):
+            nc.sync.dma_start(sbuf("wgo%d" % h, [P, JH], F32)[:], wgo[:, JH * h : JH * (h + 1)])
 
-        def load_weight_column():
-            with nc.allow_non_contiguous_dma(reason="one weight to a partition"):
-                engines[OPT["q_wcol"]].dma_start(sb("w_col", [P, JH // P], F32)[:], wgo[0, 0:JH].rearrange("(b p) -> p b", p=P))
+        load_packed("wc", 0)
+        nc.sync.dma_start(lists["dst"][:], offs2)
+        nc.sync.dma_start(lists["src"][:], offs)
+        load_scales("tab", range(4))
+        load_table(0)
+        load_float("wa", 0, 0)
+        load_float("wa", 0, 1)
+        load_packed("wb", 0)
+        load_float("wo", 0, 0)
+        load_scales("wc", (0, 1))
+        load_table(1)
+        load_scales("wc", (2, 3))
+        load_scales("wb", range(4))
+        load_float("wo", 0, 1)
+        for a in range(PASSES):
+            load_float("wa", 1, a)
+            load_float("wo", 1, a)
+        load_edge_weights(0)
+        load_packed("wc", 1)
+        load_edge_weights(1)
+        load_packed("wb", 1)
 
-        def load_weight_rows():
-            engines[OPT["q_wgo"]].dma_start(sb("wgo_sb", [P, J], F32)[:], wgo)
+        def cast(name, g, a):
+            grouped = sbuf("grp_%s%d%d" % (name, g, a), [P, NH, PACK], BF16)
+            nc.scalar.copy(
+                grouped[:].rearrange("p (c e) i -> p c i e", e=4),
+                tiles["raw_%s%d%d" % (name, g, a)][:].rearrange("p i (c e) -> p c i e", e=4),
+            )
 
-        def spread_weights():
-            rows = bank("w_rows")
-            for b in range(JH // P):
-                nc.tensor.transpose(rows[:, P * b : P * (b + 1)], tiles["w_col"][:, b : b + 1].to_broadcast([P, P]), tiles["ident"][:])
-
-        def cast(name, nt, a):
-            t = sb("grp_%s%d" % (name, nt), [P, PASSES, P, 4], BF16)
-            source = parts[name, nt, a]
-            if OPT["cast_%s%d%d" % (name, nt, a)] == "G":
-                nc.gpsimd.tensor_scalar(t[:, a], source.rearrange("p i n -> p n i"), 1.0, 0.0, ALU.mult, ALU.add)
-            else:
-                nc.scalar.copy(t[:, a].rearrange("p (c e) i -> p c i e", e=4), source.rearrange("p i (c e) -> p c i e", e=4))
-
-        def quantise(name, nt):
-            c = sb("code_%s%d" % (name, nt), [P, PASSES * P], U32)
-            s = sb("plane_%s%d" % (name, nt), [P, PASSES * P], U8)
-            nc.vector.quantize_mx(c[:].bitcast(FP8X4), s[:], tiles["grp_%s%d" % (name, nt)][:].rearrange("p a n i -> p (a n i)"))
+        def quantise(name, g, a):
+            codes = sbuf("code_%s%d%d" % (name, g, a), [P, NH], U32)
+            plane = sbuf("plane_%s%d%d" % (name, g, a), [P, NH], U8)
+            nc.vector.quantize_mx(codes[:].bitcast(FP8X4), plane[:], tiles["grp_%s%d%d" % (name, g, a)][:].rearrange("p n i -> p (n i)"))
 
         def gather_scales(which, h):
-            t = sb("ps_%s%d" % (which, h), [P, JH], U8)
-            nc.vector.tensor_copy(t[:], tiles["s_tab"][:].bitcast(U8).indirect(offsets(which, h)))
+            picked = sbuf("ps_%s%d" % (which, h), [P, JH], U8)
+            nc.vector.tensor_copy(picked[:], tiles["s_tab"][:].bitcast(U8).indirect(offsets(which, h)))
 
         def gather_words(which, a, h):
-            t = sb("pw_%s%d%d" % (which, a, h), [P, JH], U32)
-            nc.vector.tensor_copy(t[:], tiles["tab_w%d" % a][:].bitcast(U32).indirect(offsets(which, h)))
+            picked = sbuf("pw_%s%d%d" % (which, a, h), [P, JH], U32)
+            nc.vector.tensor_copy(picked[:], tiles["tab_w%d" % a][:].bitcast(U32).indirect(offsets(which, h)))
 
-        def stationary(name, nt, a):
-            if name in floats:
-                cols = slice(P * a, P * (a + 1))
-                return tiles["code_%s%d" % (name, nt)][:, cols], tiles["plane_%s%d" % (name, nt)][:, cols]
-            return (
-                parts[name, nt, a],
-                tiles["s_" + name][:].bitcast(U8)[4 * a : P, P * nt : P * (nt + 1)],
-            )
+        def weight_operand(name, g, a):
+            if name in float_weights:
+                return tiles["code_%s%d%d" % (name, g, a)][:], tiles["plane_%s%d%d" % (name, g, a)][:]
+            return tiles["packed_%s%d" % (name, g)][:, a, :], tiles["s_" + name][:].bitcast(U8)[4 * a : P, NH * g : NH * (g + 1)]
 
         terms = {"za": (("wa", "dst"), ("wb", "src")), "ms": (("wc", "src"),), "ow": (("wo", "dst"),)}
 
         def product(kind, u):
-            nt, h = UNITS[u]
-            acc = bank("%s%d" % (kind, u))
-            steps = [(name, which, a) for a in range(PASSES) for name, which in terms[kind]]
-            for i, (name, which, a) in enumerate(steps):
-                codes, plane = stationary(name, nt, a)
-                nc.tensor.matmul_mx(
-                    acc[:],
-                    lhsT=codes.bitcast(FP8X4),
-                    lhsT_scale=plane,
-                    rhs=tiles["pw_%s%d%d" % (which, a, h)][:].bitcast(FP8X4),
-                    rhs_scale=tiles["ps_%s%d" % (which, h)][4 * a : P, :],
-                    start=(i == 0),
-                    stop=(i == len(steps) - 1),
-                )
+            g, h, pair = UNITS[u]
+            acc = next_bank(kind, u)
+            passes = [(name, which, a) for a in range(PASSES) for name, which in terms[kind]]
+            for e in range(2):
+                edges = slice(P * (2 * pair + e), P * (2 * pair + e + 1))
+                for i, (name, which, a) in enumerate(passes):
+                    codes, scales = weight_operand(name, g, a)
+                    nc.tensor.matmul_mx(
+                        acc[:, NH * e : NH * (e + 1)],
+                        lhsT=tiles["pw_%s%d%d" % (which, a, h)][:, edges].bitcast(FP8X4),
+                        lhsT_scale=tiles["ps_%s%d" % (which, h)][4 * a : P, edges],
+                        rhs=codes.bitcast(FP8X4),
+                        rhs_scale=scales,
+                        start=(i == 0),
+                        stop=(i == len(passes) - 1),
+                    )
 
-        def row(kind, u):
-            return sb("%s%d" % (kind, u), [P, JH], F32)
+        def bank_copy(kind, index):
+            return sbuf("%s%d" % (kind, index), [P, BANK], F32)
 
-        def evacuate(kind, u):
-            if kind == "za":
-                nc.scalar.activation(row("eta", u)[:], tiles["za%d" % u][:], ACT.Sigmoid)
-            elif OPT[("gate%d" if kind == "ms" else "add%d") % u] == "G":
-                nc.scalar.copy(row(kind + "_sb", u)[:], tiles["%s%d" % (kind, u)][:])
+        def sigmoid(u):
+            nc.scalar.activation(bank_copy("eta", u)[:], tiles["za%d" % u][:], ACT.Sigmoid)
+
+        def copy_own(u):
+            nc.scalar.copy(bank_copy("ow_sb", u)[:], tiles["ow%d" % u][:])
 
         def gate(u):
-            e = OPT["gate%d" % u]
-            engines[e].tensor_tensor(row("msg", u)[:], tiles[("ms_sb%d" if e == "G" else "ms%d") % u][:], tiles["eta%d" % u][:], ALU.mult)
+            nc.vector.tensor_tensor(bank_copy("msg", u)[:], tiles["ms%d" % u][:], tiles["eta%d" % u][:], ALU.mult)
 
-        def add(u):
-            e = OPT["add%d" % u]
-            engines[e].tensor_tensor(row("y", u)[:], tiles[("ow_sb%d" if e == "G" else "ow%d") % u][:], tiles["msg%d" % u][:], ALU.add)
+        def turn(v):
+            acc = next_bank("y", v)
+            first_unit, t = 2 * (v // 2), v % 2
+            for b in range(JH // P):
+                channels = slice(NH * (b % 2) + P * t, NH * (b % 2) + P * (t + 1))
+                for i, kind in enumerate(("ow_sb", "msg")):
+                    nc.tensor.matmul(
+                        acc[:, P * b : P * (b + 1)],
+                        tiles["%s%d" % (kind, first_unit + b // 2)][:, channels],
+                        tiles["ident"][:],
+                        start=(i == 0),
+                        stop=(i == 1),
+                        is_transpose=True,
+                    )
 
-        def rectify(u):
-            if OPT["weigh%d" % u] != "V":
-                nc.scalar.activation(row("pos", u)[:], tiles["y%d" % u][:], ACT.Relu)
+        def relu(v):
+            nc.scalar.activation(bank_copy("pos", v)[:], tiles["y%d" % v][:], ACT.Relu)
 
-        def weigh(u):
-            h = UNITS[u][1]
-            if OPT["weigh%d" % u] == "V":
-                nc.vector.scalar_tensor_tensor(row("r", u)[:], tiles["y%d" % u][:], 0.0, tiles["w_rows"][:], ALU.max, ALU.mult)
-            elif OPT["weigh%d" % u] == "G":
-                nc.gpsimd.tensor_tensor(row("r", u)[:], tiles["pos%d" % u][:], tiles["wgo_sb"][:, JH * h : JH * (h + 1)], ALU.mult)
-
-        def scatter(u):
-            nt, h = UNITS[u]
-            window = tiles["window%d" % (nt % OPT["windows"])]
-            if OPT["weigh%d" % u] == "F":
-                nc.vector.tensor_tensor(window[:].indirect(offsets("dst", h)), tiles["pos%d" % u][:], tiles["wgo_sb"][:, JH * h : JH * (h + 1)], ALU.mult)
-            else:
-                nc.vector.tensor_copy(window[:].indirect(offsets("dst", h)), tiles["r%d" % u][:])
+        def scatter(v):
+            nt, h = PIECES[v]
+            window = tiles["window%d" % (nt % WINDOWS)]
+            nc.vector.tensor_tensor(window[:].indirect(offsets("dst", h)), tiles["pos%d" % v][:], tiles["wgo%d" % h][:], ALU.mult)
             if h == 1:
                 nc.sync.dma_start(out[P * nt : P * (nt + 1), :], window[:])
 
-        actions = {
-            "zero": zero, "warm": warm, "identity": identity, "load_list": load_list, "load_scales": load_scales,
-            "load_table": load_table, "load_float": load_float, "load_packed": load_packed,
-            "load_weight_column": load_weight_column, "load_weight_rows": load_weight_rows, "spread_weights": spread_weights,
-            "cast": cast, "quantise": quantise, "gather_scales": gather_scales, "gather_words": gather_words,
-            "product": product, "evacuate": evacuate, "gate": gate, "add": add, "rectify": rectify, "weigh": weigh, "scatter": scatter,
-        }
-        for step in STEPS:
-            actions[step[0]](*step[1:])
+        gather_scales("dst", 0)
+        gather_scales("src", 0)
+        gather_scales("src", 1)
+        gather_scales("dst", 1)
+        cast("wa", 0, 0)
+        gather_words("dst", 0, 0)
+        cast("wa", 0, 1)
+        gather_words("src", 0, 0)
+        cast("wo", 0, 0)
+        gather_words("src", 0, 1)
+        quantise("wa", 0, 0)
+        quantise("wa", 0, 1)
+        quantise("wo", 0, 0)
+        gather_words("src", 1, 0)
+        gather_words("dst", 1, 0)
+        cast("wo", 0, 1)
+
+        product("ms", 1)
+        gather_words("dst", 1, 1)
+        product("ms", 0)
+        product("za", 1)
+        quantise("wo", 0, 1)
+        gather_words("src", 1, 1)
+        sigmoid(1)
+        product("za", 0)
+        sigmoid(0)
+        product("ow", 0)
+        gate(1)
+        product("ow", 1)
+        copy_own(0)
+        product("ms", 3)
+        gate(0)
+        copy_own(1)
+        gather_words("dst", 0, 1)
+
+        cast("wa", 1, 1)
+        turn(0)
+        relu(0)
+        product("ms", 2)
+        quantise("wa", 1, 1)
+        cast("wa", 1, 0)
+        scatter(0)
+        product("ow", 2)
+        copy_own(2)
+        product("za", 2)
+        sigmoid(2)
+        product("za", 3)
+        sigmoid(3)
+        turn(1)
+        quantise("wa", 1, 0)
+        relu(1)
+        gate(2)
+        product("ms", 4)
+        cast("wo", 1, 0)
+        gate(3)
+        product("ow", 3)
+        scatter(1)
+        copy_own(3)
+
+        product("za", 4)
+        cast("wo", 1, 1)
+        turn(2)
+        sigmoid(4)
+        relu(2)
+        quantise("wo", 1, 0)
+        quantise("wo", 1, 1)
+        product("za", 5)
+        gate(4)
+        sigmoid(5)
+        product("ms", 5)
+        scatter(2)
+        turn(3)
+        relu(3)
+        product("za", 6)
+        sigmoid(6)
+        product("ms", 6)
+        product("ow", 4)
+        gate(5)
+        copy_own(4)
+        product("ow", 5)
+        scatter(3)
+        copy_own(5)
+        product("ms", 7)
+        turn(4)
+        relu(4)
+        product("za", 7)
+        gate(6)
+        sigmoid(7)
+        scatter(4)
+        turn(5)
+        relu(5)
+        product("ow", 6)
+        product("ow", 7)
+        copy_own(6)
+        copy_own(7)
+        gate(7)
+        scatter(5)
+        turn(6)
+        relu(6)
+        turn(7)
+        relu(7)
+        scatter(6)
+        scatter(7)

from contextlib import ExitStack

import concourse.mybir as mybir
from concourse.masks import make_identity

K, N, T, J = 1024, 512, 2048, 1024
FLOPS = 4 * 2 * K * N * J

F32 = mybir.dt.float32
BF16 = mybir.dt.bfloat16
I32 = mybir.dt.int32
U32 = mybir.dt.uint32
U16 = mybir.dt.uint16
U8 = mybir.dt.uint8
FP8X4 = mybir.dt.float8_e4m3fn_x4
ACT = mybir.ActivationFunctionType
ALU = mybir.AluOpType

P = 128
PACK = 4
K_PASS = P * PACK
PASSES = K // K_PASS
JH = J // 2
NH = N // 2
BANK = 512
PER_COLUMN = 16

UNITS = tuple((g, h, pair) for g in range(2) for h in range(2) for pair in range(2))
PIECES = tuple((2 * g + t, h) for g in range(2) for h in range(2) for t in range(2))

BANKS = {"za": (0, 2), "ms": (2, 3), "ow": (5, 2), "y": (7, 1)}

WINDOWS = 2

TAKES_BYTES_OF = {
    "pw_src11": "raw_wo01",
    "pw_dst01": "eta0",
    "grp_wo10": "msg1",
    "grp_wo11": "plane_wo01",
}


def tile_list_rgg_ownrelu_kernel(
    tc, tab_words, tab_scales, wa, wb_words, wb_scales, wc_words, wc_scales, wo, wgo, offs, offs2, out
):
    nc = tc.nc
    with ExitStack() as ctx:
        keep = ctx.enter_context(tc.tile_pool(name="keep", bufs=1))
        psum = ctx.enter_context(tc.psum_pool(name="psum", bufs=1))
        tiles = {}
        banks_taken = {kind: 0 for kind in BANKS}

        def sbuf(name, shape, dtype):
            tiles[name] = keep.tile(shape, dtype, name=name, tag=TAKES_BYTES_OF.get(name, name), align_bytes=64)
            return tiles[name]

        def next_bank(kind, index):
            first, count = BANKS[kind]
            name = "%s%d" % (kind, index)
            tiles[name] = psum.tile([P, BANK], F32, name=name, tag="bank%d" % (first + banks_taken[kind] % count))
            banks_taken[kind] += 1
            return tiles[name]

        lists = {
            "src": keep.tile([P, J // PER_COLUMN], U16, name="list_src"),
            "dst": keep.tile([P, J // PER_COLUMN], U16, name="list_dst"),
        }
        float_weights = {"wa": wa, "wo": wo}
        packed_weights = {"wb": wb_words, "wc": wc_words}
        scale_rows = {"tab": tab_scales, "wb": wb_scales, "wc": wc_scales}

        def offsets(which, h):
            return lists[which][:, (JH // PER_COLUMN) * h : (JH // PER_COLUMN) * (h + 1)]

        nc.vector.memset(sbuf("s_tab", [P, T // 4], I32)[:], 0)
        nc.gpsimd.memset(sbuf("window0", [P, T], F32)[:].bitcast(I32), 0)
        make_identity(nc, sbuf("ident", [P, P], F32)[:])
        nc.gpsimd.memset(sbuf("s_wc", [P, N // 4], I32)[:], 0)
        nc.gpsimd.memset(sbuf("s_wb", [P, N // 4], I32)[:], 0)
        nc.gpsimd.memset(sbuf("window1", [P, T], F32)[:].bitcast(I32), 0)

        def load_scales(name, quadrants):
            for quadrant in quadrants:
                nc.sync.dma_start(
                    tiles["s_" + name][32 * quadrant : 32 * quadrant + 4 * PASSES, :],
                    scale_rows[name][:, 4 * quadrant : 4 * quadrant + 4, :].bitcast(I32),
                )

        def load_table(a):
            nc.sync.dma_start(sbuf("tab_w%d" % a, [P, T], I32)[:], tab_words[a].rearrange("p t i -> p (t i)").bitcast(I32))

        def load_float(name, g, a):
            rows = float_weights[name][K_PASS * a : K_PASS * (a + 1), NH * g : NH * (g + 1)]
            nc.sync.dma_start(sbuf("raw_%s%d%d" % (name, g, a), [P, PACK, NH], F32)[:], rows.rearrange("(p i) n -> p i n", i=PACK))

        def load_packed(name, g):
            codes = packed_weights[name].rearrange("a p n i -> p a (n i)")[:, :, PACK * NH * g : PACK * NH * (g + 1)]
            nc.sync.dma_start(sbuf("packed_%s%d" % (name, g), [P, PASSES, NH], I32)[:], codes.bitcast(I32))

        def load_edge_weights(h):
            nc.sync.dma_start(sbuf("wgo%d" % h, [P, JH], F32)[:], wgo[:, JH * h : JH * (h + 1)])

        load_packed("wc", 0)
        nc.sync.dma_start(lists["dst"][:], offs2)
        nc.sync.dma_start(lists["src"][:], offs)
        load_scales("tab", range(4))
        load_table(0)
        load_float("wa", 0, 0)
        load_float("wa", 0, 1)
        load_packed("wb", 0)
        load_float("wo", 0, 0)
        load_scales("wc", (0, 1))
        load_table(1)
        load_scales("wc", (2, 3))
        load_scales("wb", range(4))
        load_float("wo", 0, 1)
        for a in range(PASSES):
            load_float("wa", 1, a)
            load_float("wo", 1, a)
        load_edge_weights(0)
        load_packed("wc", 1)
        load_edge_weights(1)
        load_packed("wb", 1)

        def cast(name, g, a):
            grouped = sbuf("grp_%s%d%d" % (name, g, a), [P, NH, PACK], BF16)
            nc.scalar.copy(
                grouped[:].rearrange("p (c e) i -> p c i e", e=4),
                tiles["raw_%s%d%d" % (name, g, a)][:].rearrange("p i (c e) -> p c i e", e=4),
            )

        def quantise(name, g, a):
            codes = sbuf("code_%s%d%d" % (name, g, a), [P, NH], U32)
            plane = sbuf("plane_%s%d%d" % (name, g, a), [P, NH], U8)
            nc.vector.quantize_mx(codes[:].bitcast(FP8X4), plane[:], tiles["grp_%s%d%d" % (name, g, a)][:].rearrange("p n i -> p (n i)"))

        def gather_scales(which, h):
            picked = sbuf("ps_%s%d" % (which, h), [P, JH], U8)
            nc.vector.tensor_copy(picked[:], tiles["s_tab"][:].bitcast(U8).indirect(offsets(which, h)))

        def gather_words(which, a, h):
            picked = sbuf("pw_%s%d%d" % (which, a, h), [P, JH], U32)
            nc.vector.tensor_copy(picked[:], tiles["tab_w%d" % a][:].bitcast(U32).indirect(offsets(which, h)))

        def weight_operand(name, g, a):
            if name in float_weights:
                return tiles["code_%s%d%d" % (name, g, a)][:], tiles["plane_%s%d%d" % (name, g, a)][:]
            return tiles["packed_%s%d" % (name, g)][:, a, :], tiles["s_" + name][:].bitcast(U8)[4 * a : P, NH * g : NH * (g + 1)]

        terms = {"za": (("wa", "dst"), ("wb", "src")), "ms": (("wc", "src"),), "ow": (("wo", "dst"),)}

        def product(kind, u):
            g, h, pair = UNITS[u]
            acc = next_bank(kind, u)
            passes = [(name, which, a) for a in range(PASSES) for name, which in terms[kind]]
            for e in range(2):
                edges = slice(P * (2 * pair + e), P * (2 * pair + e + 1))
                for i, (name, which, a) in enumerate(passes):
                    codes, scales = weight_operand(name, g, a)
                    nc.tensor.matmul_mx(
                        acc[:, NH * e : NH * (e + 1)],
                        lhsT=tiles["pw_%s%d%d" % (which, a, h)][:, edges].bitcast(FP8X4),
                        lhsT_scale=tiles["ps_%s%d" % (which, h)][4 * a : P, edges],
                        rhs=codes.bitcast(FP8X4),
                        rhs_scale=scales,
                        start=(i == 0),
                        stop=(i == len(passes) - 1),
                    )

        def bank_copy(kind, index):
            return sbuf("%s%d" % (kind, index), [P, BANK], F32)

        def sigmoid(u):
            nc.scalar.activation(bank_copy("eta", u)[:], tiles["za%d" % u][:], ACT.Sigmoid)

        def copy_own(u):
            nc.scalar.copy(bank_copy("ow_sb", u)[:], tiles["ow%d" % u][:])

        def gate(u):
            nc.vector.tensor_tensor(bank_copy("msg", u)[:], tiles["ms%d" % u][:], tiles["eta%d" % u][:], ALU.mult)

        def turn(v):
            acc = next_bank("y", v)
            first_unit, t = 2 * (v // 2), v % 2
            for b in range(JH // P):
                channels = slice(NH * (b % 2) + P * t, NH * (b % 2) + P * (t + 1))
                for i, kind in enumerate(("ow_sb", "msg")):
                    nc.tensor.matmul(
                        acc[:, P * b : P * (b + 1)],
                        tiles["%s%d" % (kind, first_unit + b // 2)][:, channels],
                        tiles["ident"][:],
                        start=(i == 0),
                        stop=(i == 1),
                        is_transpose=True,
                    )

        def relu(v):
            nc.scalar.activation(bank_copy("pos", v)[:], tiles["y%d" % v][:], ACT.Relu)

        def scatter(v):
            nt, h = PIECES[v]
            window = tiles["window%d" % (nt % WINDOWS)]
            nc.vector.tensor_tensor(window[:].indirect(offsets("dst", h)), tiles["pos%d" % v][:], tiles["wgo%d" % h][:], ALU.mult)
            if h == 1:
                nc.sync.dma_start(out[P * nt : P * (nt + 1), :], window[:])

        gather_scales("dst", 0)
        gather_scales("src", 0)
        gather_scales("src", 1)
        gather_scales("dst", 1)
        cast("wa", 0, 0)
        gather_words("dst", 0, 0)
        cast("wa", 0, 1)
        gather_words("src", 0, 0)
        cast("wo", 0, 0)
        gather_words("src", 0, 1)
        quantise("wa", 0, 0)
        quantise("wa", 0, 1)
        quantise("wo", 0, 0)
        gather_words("src", 1, 0)
        gather_words("dst", 1, 0)
        cast("wo", 0, 1)

        product("ms", 1)
        gather_words("dst", 1, 1)
        product("ms", 0)
        product("za", 1)
        quantise("wo", 0, 1)
        gather_words("src", 1, 1)
        sigmoid(1)
        product("za", 0)
        sigmoid(0)
        product("ow", 0)
        gate(1)
        product("ow", 1)
        copy_own(0)
        product("ms", 3)
        gate(0)
        copy_own(1)
        gather_words("dst", 0, 1)

        cast("wa", 1, 1)
        turn(0)
        relu(0)
        product("ms", 2)
        quantise("wa", 1, 1)
        cast("wa", 1, 0)
        scatter(0)
        product("ow", 2)
        copy_own(2)
        product("za", 2)
        sigmoid(2)
        product("za", 3)
        sigmoid(3)
        turn(1)
        quantise("wa", 1, 0)
        relu(1)
        gate(2)
        product("ms", 4)
        cast("wo", 1, 0)
        gate(3)
        product("ow", 3)
        scatter(1)
        copy_own(3)

        product("za", 4)
        cast("wo", 1, 1)
        turn(2)
        sigmoid(4)
        relu(2)
        quantise("wo", 1, 0)
        quantise("wo", 1, 1)
        product("za", 5)
        gate(4)
        sigmoid(5)
        product("ms", 5)
        scatter(2)
        turn(3)
        relu(3)
        product("za", 6)
        sigmoid(6)
        product("ms", 6)
        product("ow", 4)
        gate(5)
        copy_own(4)
        product("ow", 5)
        scatter(3)
        copy_own(5)
        product("ms", 7)
        turn(4)
        relu(4)
        product("za", 7)
        gate(6)
        sigmoid(7)
        scatter(4)
        turn(5)
        relu(5)
        product("ow", 6)
        product("ow", 7)
        copy_own(6)
        copy_own(7)
        gate(7)
        scatter(5)
        turn(6)
        relu(6)
        turn(7)
        relu(7)
        scatter(6)
        scatter(7)
